import numpy as np
import ml_dtypes


def mxq(x, axis, fmt="e4m3"):
    dtype, down = {"e4m3": (ml_dtypes.float8_e4m3fn, 7), "e5m2": (ml_dtypes.float8_e5m2, 14)}[fmt]
    v = np.moveaxis(np.asarray(x, np.float32).astype(ml_dtypes.bfloat16).astype(np.float64), axis, -1)
    blocks = v.reshape(v.shape[:-1] + (-1, 32))
    amax = np.abs(blocks).max(-1, keepdims=True)
    byte = np.maximum(np.where(amax > 0, np.frexp(amax)[1] - 1 + 127, 0) - down, 1)
    scale = np.exp2(byte - 127.0)
    codes = (blocks / scale).astype(np.float32).astype(dtype).astype(np.float64)
    return np.moveaxis((codes * scale).reshape(v.shape), -1, axis)


WIDE = False


def mx_kscale(k):
    if not WIDE:
        return np.ones(k)
    levels = np.array([10, -10, 5, -5, 0])
    if k % 512:
        return np.exp2(np.random.permutation(np.resize(levels, k // 32))).repeat(32)
    a = np.empty((k // 512, 16))
    for p in range(k // 512):
        a[p, :8] = np.random.permutation(np.resize(levels, 8))
        for g in range(8):
            far = levels[np.abs(levels - a[p, g]) >= 10]
            a[p, g + 8] = far[np.random.randint(len(far))]
    return np.exp2(a.ravel()).repeat(32)


def f64(x):
    return np.asarray(x).astype(np.float64)


def striped(idx):
    return np.tile(idx.reshape(-1, 16).T, (8, 1)).astype(np.uint16)


def unstriped(offs):
    return offs[:16].T.reshape(-1).astype(np.int64)


E2M1 = np.array([0.0, 0.5, 1.0, 1.5, 2.0, 3.0, 4.0, 6.0, -0.0, -0.5, -1.0, -1.5, -2.0, -3.0, -4.0, -6.0])


def pack_weight(w, fmt):
    k, n = w.shape
    w = f64(np.asarray(w, np.float32).astype(ml_dtypes.bfloat16)).reshape(k // 32, 32, n)
    amax = np.abs(w).max(1)
    if fmt == "e4m3":
        byte = np.frexp(amax)[1] - 1 + 127 - 7
    else:
        mant, ex = np.frexp(amax / 6.0)
        byte = np.where(mant > 0.5, ex, ex - 1) + 127
    byte = np.clip(np.where(amax > 0, byte, 1), 1, 254)
    scaled = (w * np.exp2(127.0 - byte)[:, None, :]).reshape(k, n).astype(np.float32)
    by_word = np.ascontiguousarray(scaled.reshape(k // 512, 128, 4, n).transpose(0, 1, 3, 2))
    if fmt == "e4m3":
        words = by_word.astype(ml_dtypes.float8_e4m3fn).view(np.uint8)
    else:
        c = by_word.astype(ml_dtypes.float4_e2m1fn).view(np.uint8) & 0xF
        words = (c[..., 0::2] | (c[..., 1::2] << 4)).reshape(k // 512, 128, 2 * n)
    return np.ascontiguousarray(words), np.ascontiguousarray(byte.astype(np.uint8).reshape(k // 512, 16, n))


def unpack_weight(words, scales, fmt):
    g, _, n = scales.shape
    words = np.ascontiguousarray(words).reshape(g, 128, n, -1)
    if fmt == "e4m3":
        vals = words.view(ml_dtypes.float8_e4m3fn).astype(np.float64)
    else:
        nib = np.empty((g, 128, n, 4), np.uint8)
        nib[..., 0::2] = words & 0xF
        nib[..., 1::2] = words >> 4
        vals = E2M1[nib]
    vals = vals * np.repeat(np.exp2(scales.astype(np.float64) - 127.0), 8, axis=1)[..., None]
    return vals.transpose(0, 1, 3, 2).reshape(g * 512, n)


K, M, T, S = 1024, 512, 2048, 1024


def setup_inputs():
    n = np.random.standard_normal
    s = mx_kscale(K)[:, None]
    w = n((K, M)) / np.sqrt(K) / s
    v = pack_weight(n((K, T)) * s, "e4m3")
    p_w4 = pack_weight(w[512:], "e2m1")
    return {
        "tab_words": v[0],
        "tab_scales": v[1],
        "w8": (w[:512]).astype(np.float32),
        "w4_words": p_w4[0],
        "w4_scales": p_w4[1],
        "rT": n((M, T)).astype(np.float32),
        "offs": striped(np.random.permutation(T)[:S]),
    }


def reference(tab_words, tab_scales, w8, w4_words, w4_scales, rT, offs):
    tab_ = unpack_weight(tab_words, tab_scales, "e4m3")[:, unstriped(offs)]
    w8_ = mxq(f64(w8), 0, "e4m3")
    w4_ = unpack_weight(w4_words, w4_scales, "e2m1")
    y = w8_.T @ tab_[:512] + w4_.T @ tab_[512:]
    return (y) + f64(rT)[:, unstriped(offs)]

@@ -1,0 +1,135 @@
+from contextlib import ExitStack
+
+import concourse.mybir as mybir
+
+K, M, T, S = 1024, 512, 2048, 1024
+FLOPS = 2 * K * M * S
+
+F32 = mybir.dt.float32
+BF16 = mybir.dt.bfloat16
+I32 = mybir.dt.int32
+U32 = mybir.dt.uint32
+U16 = mybir.dt.uint16
+U8 = mybir.dt.uint8
+FP8X4 = mybir.dt.float8_e4m3fn_x4
+FP4X4 = mybir.dt.float4_e2m1fn_x4
+ADD = mybir.AluOpType.add
+
+P = 128
+PACK = 4
+N_TILE = 512
+ROW_TILES = M // P
+PLANE0 = 12
+
+SCALE_LOADS = [(0, 16, 4), (12, 0, 32), (44, 4, 4), (64, 24, 4), (68, 0, 32), (108, 12, 4)]
+
+
+def tile_list_tabres_none_kernel(
+    tc, tab_words, tab_scales, w8, w4_words, w4_scales, rT, offs, out
+):
+    nc = tc.nc
+    with ExitStack() as ctx:
+        keep = ctx.enter_context(tc.tile_pool(name="keep", bufs=1))
+        psum = ctx.enter_context(tc.psum_pool(name="psum", bufs=1))
+
+        offsets = keep.tile([P, S // 16], U16, name="offsets")
+        words = [keep.tile([P, T], I32, name=f"words{a}") for a in range(2)]
+        scales = keep.tile([P, T // 4], I32, name="scales")
+        w8_raw = keep.tile([P, PACK, M], F32, name="w8_raw")
+        w4_codes = keep.tile([P, 2 * M], U8, name="w4_codes", align_bytes=64)
+        w4_plane = keep.tile([P, M // 4], I32, name="w4_plane", align_bytes=64)
+        resid = [keep.tile([P, T], F32, name=f"resid{m}") for m in range(ROW_TILES)]
+
+        nc.vector.memset(scales[:], 0)
+        nc.vector.memset(w4_plane[:], 0)
+
+        nc.sync.dma_start(offsets[:], offs)
+        nc.sync.dma_start(words[0][:], tab_words[0].rearrange("p t i -> p (t i)").bitcast(I32))
+        scale_rows = tab_scales.rearrange("a q t -> (a q) t").bitcast(I32)
+        for part, row, count in SCALE_LOADS:
+            nc.scalar.dma_start(scales[part : part + count, :], scale_rows[row : row + count, :])
+        nc.sync.dma_start(words[1][:], tab_words[1].rearrange("p t i -> p (t i)").bitcast(I32))
+        nc.sync.dma_start(w8_raw[:], w8.rearrange("(p j) n -> p j n", j=PACK))
+        nc.sync.dma_start(resid[0][:], rT[0:P, :])
+        nc.sync.dma_start(w4_codes[:].bitcast(I32), w4_words[0].bitcast(I32))
+        w4_rows = w4_scales[0].bitcast(I32)
+        for q in range(4):
+            nc.sync.dma_start(w4_plane[32 * q : 32 * q + 4, :], w4_rows[4 * q : 4 * q + 4, :])
+        for m in range(1, ROW_TILES):
+            nc.sync.dma_start(resid[m][:], rT[m * P : (m + 1) * P, :])
+
+        picked_scales = keep.tile([P, S], U8, name="picked_scales", align_bytes=64)
+        picked_words = [keep.tile([P, S], U32, name=f"picked_words{a}", align_bytes=64) for a in range(2)]
+        nc.vector.tensor_copy(picked_scales[:], scales[:].bitcast(U8).indirect(offsets[:]))
+        for a in range(2):
+            nc.vector.tensor_copy(picked_words[a][:], words[a][:].bitcast(U32).indirect(offsets[:]))
+
+        grouped = [keep.tile([P, P, PACK], BF16, name=f"grouped{m}", align_bytes=64) for m in range(ROW_TILES)]
+        w8_codes = [keep.tile([P, P], U32, name=f"w8_codes{m}", align_bytes=64) for m in range(ROW_TILES)]
+        w8_plane = [keep.tile([P, P], U8, name=f"w8_plane{m}", align_bytes=64) for m in range(ROW_TILES)]
+        for m in range(ROW_TILES):
+            dst = grouped[m][:].rearrange("p (c i) t -> p c t i", i=4)
+            src = w8_raw[:, :, m * P : (m + 1) * P].rearrange("p t (c i) -> p c t i", i=4)
+            if m == ROW_TILES - 1:
+                nc.vector.tensor_copy(dst, src)
+            else:
+                nc.scalar.copy(dst, src)
+        for m in range(ROW_TILES):
+            nc.vector.quantize_mx(
+                out=w8_codes[m][:].bitcast(FP8X4),
+                scales=w8_plane[m][:],
+                in_=grouped[m][:].rearrange("p c t -> p (c t)"),
+            )
+
+        banks = {}
+        for m in range(ROW_TILES):
+            for h in range(S // N_TILE):
+                cols = slice(h * N_TILE, (h + 1) * N_TILE)
+                acc = psum.tile([P, N_TILE], F32, name=f"acc{m}_{h}")
+                banks[m, h] = acc
+                nc.tensor.matmul_mx(
+                    out=acc[:],
+                    lhsT=w8_codes[m][:].bitcast(FP8X4),
+                    lhsT_scale=w8_plane[m][:],
+                    rhs=picked_words[0][:, cols].bitcast(FP8X4),
+                    rhs_scale=picked_scales[PLANE0:P, cols],
+                    start=True,
+                    stop=False,
+                )
+                nc.tensor.matmul_mx(
+                    out=acc[:],
+                    lhsT=w4_codes[:, 2 * m * P : 2 * (m + 1) * P].bitcast(FP4X4),
+                    lhsT_scale=w4_plane[:].bitcast(U8)[:, m * P : (m + 1) * P],
+                    rhs=picked_words[1][:, cols].bitcast(FP8X4),
+                    rhs_scale=picked_scales[:, cols],
+                    start=False,
+                    stop=True,
+                )
+
+        for m in range(ROW_TILES):
+            width = S if m < ROW_TILES - 1 else 256
+            piece = N_TILE if m < ROW_TILES - 1 else 256
+            gathered = []
+            for g0 in range(0, S, width):
+                picked = keep.tile([P, width], F32, name=f"picked{m}_{g0}")
+                gathered.append((g0, picked))
+
+            def gather(i):
+                g0, picked = gathered[i]
+                nc.vector.tensor_copy(picked[:], resid[m][:].indirect(offsets[:, g0 // 16 : (g0 + width) // 16]))
+
+            def finish(i):
+                g0, picked = gathered[i]
+                for c0 in range(g0, g0 + width, piece):
+                    result = keep.tile([P, piece], F32, name=f"result{m}_{c0}")
+                    h, b0 = divmod(c0, N_TILE)
+                    nc.vector.tensor_tensor(
+                        result[:], banks[m, h][:, b0 : b0 + piece], picked[:, c0 - g0 : c0 - g0 + piece], ADD
+                    )
+                    nc.sync.dma_start(out[m * P : (m + 1) * P, c0 : c0 + piece], result[:])
+
+            gather(0)
+            for i in range(1, len(gathered)):
+                gather(i)
+                finish(i - 1)
+            finish(len(gathered) - 1)

@@ -21,7 +21,7 @@ N_TILE = 512
 ROW_TILES = M // P
 PLANE0 = 12
 
-SCALE_LOADS = [(0, 16, 4), (12, 0, 32), (44, 4, 4), (64, 24, 4), (68, 0, 32), (108, 12, 4)]
+SCALE_LOADS = [(0, 16, 12), (12, 0, 32), (44, 4, 24), (68, 0, 32), (100, 4, 28)]
 
 
 def tile_list_tabres_none_kernel(
@@ -33,103 +33,99 @@ def tile_list_tabres_none_kernel(
         psum = ctx.enter_context(tc.psum_pool(name="psum", bufs=1))
 
         offsets = keep.tile([P, S // 16], U16, name="offsets")
-        words = [keep.tile([P, T], I32, name=f"words{a}") for a in range(2)]
         scales = keep.tile([P, T // 4], I32, name="scales")
         w8_raw = keep.tile([P, PACK, M], F32, name="w8_raw")
+        words = [keep.tile([P, T], I32, name=f"words{a}") for a in range(2)]
         w4_codes = keep.tile([P, 2 * M], U8, name="w4_codes", align_bytes=64)
         w4_plane = keep.tile([P, M // 4], I32, name="w4_plane", align_bytes=64)
         resid = [keep.tile([P, T], F32, name=f"resid{m}") for m in range(ROW_TILES)]
 
-        nc.vector.memset(scales[:], 0)
-        nc.vector.memset(w4_plane[:], 0)
+        nc.gpsimd.memset(w4_plane[:], 0)
 
-        nc.sync.dma_start(offsets[:], offs)
-        nc.sync.dma_start(words[0][:], tab_words[0].rearrange("p t i -> p (t i)").bitcast(I32))
+        table_words = [tab_words[a].rearrange("p t i -> p (t i)").bitcast(I32) for a in range(2)]
         scale_rows = tab_scales.rearrange("a q t -> (a q) t").bitcast(I32)
-        for part, row, count in SCALE_LOADS:
-            nc.scalar.dma_start(scales[part : part + count, :], scale_rows[row : row + count, :])
-        nc.sync.dma_start(words[1][:], tab_words[1].rearrange("p t i -> p (t i)").bitcast(I32))
-        nc.sync.dma_start(w8_raw[:], w8.rearrange("(p j) n -> p j n", j=PACK))
-        nc.sync.dma_start(resid[0][:], rT[0:P, :])
-        nc.sync.dma_start(w4_codes[:].bitcast(I32), w4_words[0].bitcast(I32))
         w4_rows = w4_scales[0].bitcast(I32)
+        nc.sync.dma_start(offsets[:], offs)
+        nc.sync.dma_start(words[1][:], table_words[1])
+        for part, row, count in SCALE_LOADS:
+            nc.sync.dma_start(scales[part : part + count, :], scale_rows[row : row + count, :])
+        nc.sync.dma_start(w8_raw[:], w8.rearrange("(p j) n -> p j n", j=PACK))
+        nc.sync.dma_start(w4_codes[:].bitcast(I32), w4_words[0].bitcast(I32))
         for q in range(4):
             nc.sync.dma_start(w4_plane[32 * q : 32 * q + 4, :], w4_rows[4 * q : 4 * q + 4, :])
-        for m in range(1, ROW_TILES):
+        nc.sync.dma_start(words[0][:], table_words[0])
+        for m in range(ROW_TILES):
             nc.sync.dma_start(resid[m][:], rT[m * P : (m + 1) * P, :])
 
         picked_scales = keep.tile([P, S], U8, name="picked_scales", align_bytes=64)
         picked_words = [keep.tile([P, S], U32, name=f"picked_words{a}", align_bytes=64) for a in range(2)]
+        nc.vector.tensor_copy(picked_words[1][:], words[1][:].bitcast(U32).indirect(offsets[:]))
         nc.vector.tensor_copy(picked_scales[:], scales[:].bitcast(U8).indirect(offsets[:]))
-        for a in range(2):
-            nc.vector.tensor_copy(picked_words[a][:], words[a][:].bitcast(U32).indirect(offsets[:]))
 
-        grouped = [keep.tile([P, P, PACK], BF16, name=f"grouped{m}", align_bytes=64) for m in range(ROW_TILES)]
-        w8_codes = [keep.tile([P, P], U32, name=f"w8_codes{m}", align_bytes=64) for m in range(ROW_TILES)]
-        w8_plane = [keep.tile([P, P], U8, name=f"w8_plane{m}", align_bytes=64) for m in range(ROW_TILES)]
-        for m in range(ROW_TILES):
-            dst = grouped[m][:].rearrange("p (c i) t -> p c t i", i=4)
-            src = w8_raw[:, :, m * P : (m + 1) * P].rearrange("p t (c i) -> p c t i", i=4)
-            if m == ROW_TILES - 1:
-                nc.vector.tensor_copy(dst, src)
-            else:
-                nc.scalar.copy(dst, src)
-        for m in range(ROW_TILES):
+        half = M // 2
+        grouped = [keep.tile([P, half, PACK], BF16, name=f"grouped{u}", align_bytes=64) for u in range(2)]
+        w8_codes = keep.tile([P, M], U32, name="w8_codes", align_bytes=64)
+        w8_plane = keep.tile([P, M], U8, name="w8_plane", align_bytes=64)
+        for u in range(2):
+            cols = slice(u * half, (u + 1) * half)
+            nc.scalar.copy(
+                grouped[u][:].rearrange("p (c i) t -> p c t i", i=4),
+                w8_raw[:, :, cols].rearrange("p t (c i) -> p c t i", i=4),
+            )
             nc.vector.quantize_mx(
-                out=w8_codes[m][:].bitcast(FP8X4),
-                scales=w8_plane[m][:],
-                in_=grouped[m][:].rearrange("p c t -> p (c t)"),
+                out=w8_codes[:, cols].bitcast(FP8X4),
+                scales=w8_plane[:, cols],
+                in_=grouped[u][:].rearrange("p c t -> p (c t)"),
+            )
+        for h in range(S // N_TILE):
+            nc.vector.tensor_copy(
+                picked_words[0][:, h * N_TILE : (h + 1) * N_TILE],
+                words[0][:].bitcast(U32).indirect(offsets[:, h * N_TILE // 16 : (h + 1) * N_TILE // 16]),
             )
 
         banks = {}
         for m in range(ROW_TILES):
             for h in range(S // N_TILE):
                 cols = slice(h * N_TILE, (h + 1) * N_TILE)
-                acc = psum.tile([P, N_TILE], F32, name=f"acc{m}_{h}")
-                banks[m, h] = acc
+                banks[m, h] = psum.tile([P, N_TILE], F32, name=f"acc{m}_{h}")
                 nc.tensor.matmul_mx(
-                    out=acc[:],
-                    lhsT=w8_codes[m][:].bitcast(FP8X4),
-                    lhsT_scale=w8_plane[m][:],
-                    rhs=picked_words[0][:, cols].bitcast(FP8X4),
-                    rhs_scale=picked_scales[PLANE0:P, cols],
-                    start=True,
-                    stop=False,
-                )
-                nc.tensor.matmul_mx(
-                    out=acc[:],
+                    out=banks[m, h][:],
                     lhsT=w4_codes[:, 2 * m * P : 2 * (m + 1) * P].bitcast(FP4X4),
                     lhsT_scale=w4_plane[:].bitcast(U8)[:, m * P : (m + 1) * P],
                     rhs=picked_words[1][:, cols].bitcast(FP8X4),
                     rhs_scale=picked_scales[:, cols],
+                    start=True,
+                    stop=False,
+                )
+        for m in range(ROW_TILES):
+            for h in range(S // N_TILE):
+                cols = slice(h * N_TILE, (h + 1) * N_TILE)
+                nc.tensor.matmul_mx(
+                    out=banks[m, h][:],
+                    lhsT=w8_codes[:, m * P : (m + 1) * P].bitcast(FP8X4),
+                    lhsT_scale=w8_plane[:, m * P : (m + 1) * P],
+                    rhs=picked_words[0][:, cols].bitcast(FP8X4),
+                    rhs_scale=picked_scales[PLANE0:P, cols],
                     start=False,
                     stop=True,
                 )
 
         for m in range(ROW_TILES):
-            width = S if m < ROW_TILES - 1 else 256
-            piece = N_TILE if m < ROW_TILES - 1 else 256
-            gathered = []
-            for g0 in range(0, S, width):
-                picked = keep.tile([P, width], F32, name=f"picked{m}_{g0}")
-                gathered.append((g0, picked))
-
-            def gather(i):
-                g0, picked = gathered[i]
-                nc.vector.tensor_copy(picked[:], resid[m][:].indirect(offsets[:, g0 // 16 : (g0 + width) // 16]))
-
-            def finish(i):
-                g0, picked = gathered[i]
-                for c0 in range(g0, g0 + width, piece):
-                    result = keep.tile([P, piece], F32, name=f"result{m}_{c0}")
-                    h, b0 = divmod(c0, N_TILE)
-                    nc.vector.tensor_tensor(
-                        result[:], banks[m, h][:, b0 : b0 + piece], picked[:, c0 - g0 : c0 - g0 + piece], ADD
-                    )
-                    nc.sync.dma_start(out[m * P : (m + 1) * P, c0 : c0 + piece], result[:])
-
-            gather(0)
-            for i in range(1, len(gathered)):
-                gather(i)
-                finish(i - 1)
-            finish(len(gathered) - 1)
+            rows = slice(m * P, (m + 1) * P)
+            for h in range(S // N_TILE):
+                last = m == ROW_TILES - 1 and h == S // N_TILE - 1
+                width = 256 if last else N_TILE
+                starts = range(h * N_TILE, (h + 1) * N_TILE, width)
+                picked = {c0: keep.tile([P, width], F32, name=f"picked{m}_{c0}") for c0 in starts}
+                for c0 in starts:
+                    nc.vector.tensor_copy(picked[c0][:], resid[m][:].indirect(offsets[:, c0 // 16 : (c0 + width) // 16]))
+                for c0 in starts:
+                    result = keep.tile([P, width], F32, name=f"result{m}_{c0}")
+                    y = banks[m, h][:, c0 - h * N_TILE : c0 - h * N_TILE + width]
+                    if last:
+                        nc.vector.tensor_tensor(result[:], y, picked[c0][:], ADD)
+                    else:
+                        y_sb = keep.tile([P, width], F32, name=f"y_sb{m}_{c0}")
+                        nc.scalar.copy(y_sb[:], y)
+                        nc.gpsimd.tensor_tensor(result[:], y_sb[:], picked[c0][:], ADD)
+                    nc.sync.dma_start(out[rows, c0 : c0 + width], result[:])

@@ -30,7 +30,7 @@ def tile_list_tabres_none_kernel(
     nc = tc.nc
     with ExitStack() as ctx:
         keep = ctx.enter_context(tc.tile_pool(name="keep", bufs=1))
-        psum = ctx.enter_context(tc.psum_pool(name="psum", bufs=1))
+        psum = ctx.enter_context(tc.psum_pool(name="psum", bufs=4))
 
         offsets = keep.tile([P, S // 16], U16, name="offsets")
         scales = keep.tile([P, T // 4], I32, name="scales")
@@ -41,19 +41,23 @@ def tile_list_tabres_none_kernel(
         resid = [keep.tile([P, T], F32, name=f"resid{m}") for m in range(ROW_TILES)]
 
         nc.gpsimd.memset(w4_plane[:], 0)
+        warm = keep.tile([P, 2], F32, name="warm")
+        nc.vector.memset(warm[:, 0:1], 0.0)
+        nc.scalar.copy(warm[:, 1:2], warm[:, 0:1])
 
         table_words = [tab_words[a].rearrange("p t i -> p (t i)").bitcast(I32) for a in range(2)]
         scale_rows = tab_scales.rearrange("a q t -> (a q) t").bitcast(I32)
         w4_rows = w4_scales[0].bitcast(I32)
-        nc.sync.dma_start(offsets[:], offs)
         nc.sync.dma_start(words[1][:], table_words[1])
+        nc.sync.dma_start(offsets[:], offs)
         for part, row, count in SCALE_LOADS:
-            nc.sync.dma_start(scales[part : part + count, :], scale_rows[row : row + count, :])
-        nc.sync.dma_start(w8_raw[:], w8.rearrange("(p j) n -> p j n", j=PACK))
+            queue = nc.scalar if part == 0 else nc.sync
+            queue.dma_start(scales[part : part + count, :], scale_rows[row : row + count, :])
+        nc.sync.dma_start(words[0][:], table_words[0])
         nc.sync.dma_start(w4_codes[:].bitcast(I32), w4_words[0].bitcast(I32))
         for q in range(4):
             nc.sync.dma_start(w4_plane[32 * q : 32 * q + 4, :], w4_rows[4 * q : 4 * q + 4, :])
-        nc.sync.dma_start(words[0][:], table_words[0])
+        nc.sync.dma_start(w8_raw[:], w8.rearrange("(p j) n -> p j n", j=PACK))
         for m in range(ROW_TILES):
             nc.sync.dma_start(resid[m][:], rT[m * P : (m + 1) * P, :])
 
@@ -61,6 +65,7 @@ def tile_list_tabres_none_kernel(
         picked_words = [keep.tile([P, S], U32, name=f"picked_words{a}", align_bytes=64) for a in range(2)]
         nc.vector.tensor_copy(picked_words[1][:], words[1][:].bitcast(U32).indirect(offsets[:]))
         nc.vector.tensor_copy(picked_scales[:], scales[:].bitcast(U8).indirect(offsets[:]))
+        nc.vector.tensor_copy(picked_words[0][:], words[0][:].bitcast(U32).indirect(offsets[:]))
 
         half = M // 2
         grouped = [keep.tile([P, half, PACK], BF16, name=f"grouped{u}", align_bytes=64) for u in range(2)]
@@ -77,17 +82,13 @@ def tile_list_tabres_none_kernel(
                 scales=w8_plane[:, cols],
                 in_=grouped[u][:].rearrange("p c t -> p (c t)"),
             )
-        for h in range(S // N_TILE):
-            nc.vector.tensor_copy(
-                picked_words[0][:, h * N_TILE : (h + 1) * N_TILE],
-                words[0][:].bitcast(U32).indirect(offsets[:, h * N_TILE // 16 : (h + 1) * N_TILE // 16]),
-            )
 
         banks = {}
         for m in range(ROW_TILES):
+            rows = slice(m * P, (m + 1) * P)
             for h in range(S // N_TILE):
                 cols = slice(h * N_TILE, (h + 1) * N_TILE)
-                banks[m, h] = psum.tile([P, N_TILE], F32, name=f"acc{m}_{h}")
+                banks[m, h] = psum.tile([P, N_TILE], F32, name=f"acc{m}_{h}", tag="acc")
                 nc.tensor.matmul_mx(
                     out=banks[m, h][:],
                     lhsT=w4_codes[:, 2 * m * P : 2 * (m + 1) * P].bitcast(FP4X4),
@@ -97,9 +98,6 @@ def tile_list_tabres_none_kernel(
                     start=True,
                     stop=False,
                 )
-        for m in range(ROW_TILES):
-            for h in range(S // N_TILE):
-                cols = slice(h * N_TILE, (h + 1) * N_TILE)
                 nc.tensor.matmul_mx(
                     out=banks[m, h][:],
                     lhsT=w8_codes[:, m * P : (m + 1) * P].bitcast(FP8X4),
@@ -110,22 +108,30 @@ def tile_list_tabres_none_kernel(
                     stop=True,
                 )
 
-        for m in range(ROW_TILES):
-            rows = slice(m * P, (m + 1) * P)
-            for h in range(S // N_TILE):
-                last = m == ROW_TILES - 1 and h == S // N_TILE - 1
-                width = 256 if last else N_TILE
-                starts = range(h * N_TILE, (h + 1) * N_TILE, width)
-                picked = {c0: keep.tile([P, width], F32, name=f"picked{m}_{c0}") for c0 in starts}
-                for c0 in starts:
-                    nc.vector.tensor_copy(picked[c0][:], resid[m][:].indirect(offsets[:, c0 // 16 : (c0 + width) // 16]))
-                for c0 in starts:
-                    result = keep.tile([P, width], F32, name=f"result{m}_{c0}")
-                    y = banks[m, h][:, c0 - h * N_TILE : c0 - h * N_TILE + width]
-                    if last:
-                        nc.vector.tensor_tensor(result[:], y, picked[c0][:], ADD)
-                    else:
-                        y_sb = keep.tile([P, width], F32, name=f"y_sb{m}_{c0}")
-                        nc.scalar.copy(y_sb[:], y)
-                        nc.gpsimd.tensor_tensor(result[:], y_sb[:], picked[c0][:], ADD)
+            width = N_TILE if m < ROW_TILES - 1 else 256
+
+            def gather(c0):
+                picked = keep.tile([P, width], F32, name=f"picked{m}_{c0}")
+                nc.vector.tensor_copy(picked[:], resid[m][:].indirect(offsets[:, c0 // 16 : (c0 + width) // 16]))
+                return picked
+
+            def finish(c0, picked):
+                result = keep.tile([P, width], F32, name=f"result{m}_{c0}")
+                h, b0 = divmod(c0, N_TILE)
+                y = banks[m, h][:, b0 : b0 + width]
+                if m == ROW_TILES - 1 and c0 > 0:
+                    nc.vector.tensor_tensor(result[:], y, picked[:], ADD)
+                    nc.scalar.dma_start(out[rows, c0 : c0 + width], result[:])
+                else:
+                    y_sb = keep.tile([P, width], F32, name=f"y_sb{m}_{c0}")
+                    nc.scalar.copy(y_sb[:], y)
+                    nc.gpsimd.tensor_tensor(result[:], y_sb[:], picked[:], ADD)
                     nc.sync.dma_start(out[rows, c0 : c0 + width], result[:])
+
+            before = None
+            for c0 in range(0, S, width):
+                picked = gather(c0)
+                if before is not None:
+                    finish(*before)
+                before = (c0, picked)
+            finish(*before)

@@ -20,6 +20,7 @@ PACK = 4
 N_TILE = 512
 ROW_TILES = M // P
 PLANE0 = 12
+TAIL = 256
 
 SCALE_LOADS = [(0, 16, 12), (12, 0, 32), (44, 4, 24), (68, 0, 32), (100, 4, 28)]
 
@@ -54,10 +55,10 @@ def tile_list_tabres_none_kernel(
             queue = nc.scalar if part == 0 else nc.sync
             queue.dma_start(scales[part : part + count, :], scale_rows[row : row + count, :])
         nc.sync.dma_start(words[0][:], table_words[0])
+        nc.sync.dma_start(w8_raw[:], w8.rearrange("(p j) n -> p j n", j=PACK))
         nc.sync.dma_start(w4_codes[:].bitcast(I32), w4_words[0].bitcast(I32))
         for q in range(4):
             nc.sync.dma_start(w4_plane[32 * q : 32 * q + 4, :], w4_rows[4 * q : 4 * q + 4, :])
-        nc.sync.dma_start(w8_raw[:], w8.rearrange("(p j) n -> p j n", j=PACK))
         for m in range(ROW_TILES):
             nc.sync.dma_start(resid[m][:], rT[m * P : (m + 1) * P, :])
 
@@ -108,30 +109,23 @@ def tile_list_tabres_none_kernel(
                     stop=True,
                 )
 
-            width = N_TILE if m < ROW_TILES - 1 else 256
-
-            def gather(c0):
+            def gather(c0, width):
                 picked = keep.tile([P, width], F32, name=f"picked{m}_{c0}")
                 nc.vector.tensor_copy(picked[:], resid[m][:].indirect(offsets[:, c0 // 16 : (c0 + width) // 16]))
                 return picked
 
-            def finish(c0, picked):
-                result = keep.tile([P, width], F32, name=f"result{m}_{c0}")
-                h, b0 = divmod(c0, N_TILE)
-                y = banks[m, h][:, b0 : b0 + width]
-                if m == ROW_TILES - 1 and c0 > 0:
-                    nc.vector.tensor_tensor(result[:], y, picked[:], ADD)
-                    nc.scalar.dma_start(out[rows, c0 : c0 + width], result[:])
-                else:
-                    y_sb = keep.tile([P, width], F32, name=f"y_sb{m}_{c0}")
-                    nc.scalar.copy(y_sb[:], y)
+            for h in range(S // N_TILE):
+                c0 = h * N_TILE
+                if (m, h) != (ROW_TILES - 1, S // N_TILE - 1):
+                    picked = gather(c0, N_TILE)
+                    y_sb = keep.tile([P, N_TILE], F32, name=f"y_sb{m}_{h}")
+                    nc.scalar.copy(y_sb[:], banks[m, h][:])
+                    result = keep.tile([P, N_TILE], F32, name=f"result{m}_{h}")
                     nc.gpsimd.tensor_tensor(result[:], y_sb[:], picked[:], ADD)
-                    nc.sync.dma_start(out[rows, c0 : c0 + width], result[:])
-
-            before = None
-            for c0 in range(0, S, width):
-                picked = gather(c0)
-                if before is not None:
-                    finish(*before)
-                before = (c0, picked)
-            finish(*before)
+                    nc.sync.dma_start(out[rows, c0 : c0 + N_TILE], result[:])
+                else:
+                    tail = [(b0, gather(c0 + b0, TAIL)) for b0 in range(0, N_TILE, TAIL)]
+                    for b0, picked in tail:
+                        result = keep.tile([P, TAIL], F32, name=f"tail{b0}")
+                        nc.vector.tensor_tensor(result[:], banks[m, h][:, b0 : b0 + TAIL], picked[:], ADD)
+                        nc.scalar.dma_start(out[rows, c0 + b0 : c0 + b0 + TAIL], result[:])

@@ -109,23 +109,15 @@ def tile_list_tabres_none_kernel(
                     stop=True,
                 )
 
-            def gather(c0, width):
-                picked = keep.tile([P, width], F32, name=f"picked{m}_{c0}")
-                nc.vector.tensor_copy(picked[:], resid[m][:].indirect(offsets[:, c0 // 16 : (c0 + width) // 16]))
-                return picked
-
             for h in range(S // N_TILE):
                 c0 = h * N_TILE
-                if (m, h) != (ROW_TILES - 1, S // N_TILE - 1):
-                    picked = gather(c0, N_TILE)
-                    y_sb = keep.tile([P, N_TILE], F32, name=f"y_sb{m}_{h}")
-                    nc.scalar.copy(y_sb[:], banks[m, h][:])
-                    result = keep.tile([P, N_TILE], F32, name=f"result{m}_{h}")
-                    nc.gpsimd.tensor_tensor(result[:], y_sb[:], picked[:], ADD)
-                    nc.sync.dma_start(out[rows, c0 : c0 + N_TILE], result[:])
-                else:
-                    tail = [(b0, gather(c0 + b0, TAIL)) for b0 in range(0, N_TILE, TAIL)]
-                    for b0, picked in tail:
-                        result = keep.tile([P, TAIL], F32, name=f"tail{b0}")
-                        nc.vector.tensor_tensor(result[:], banks[m, h][:, b0 : b0 + TAIL], picked[:], ADD)
-                        nc.scalar.dma_start(out[rows, c0 + b0 : c0 + b0 + TAIL], result[:])
+                y_sb = keep.tile([P, N_TILE], F32, name=f"y_sb{m}_{h}")
+                nc.scalar.copy(y_sb[:], banks[m, h][:])
+                last = (m, h) == (ROW_TILES - 1, S // N_TILE - 1)
+                width = TAIL if last else N_TILE
+                for b0 in range(0, N_TILE, width):
+                    result = keep.tile([P, width], F32, name=f"result{m}_{h}_{b0}")
+                    picks = offsets[:, (c0 + b0) // 16 : (c0 + b0 + width) // 16]
+                    nc.vector.tensor_tensor(result[:], resid[m][:].indirect(picks), y_sb[:, b0 : b0 + width], ADD)
+                    queue = nc.scalar if last else nc.sync
+                    queue.dma_start(out[rows, c0 + b0 : c0 + b0 + width], result[:])

@@ -22,7 +22,9 @@ ROW_TILES = M // P
 PLANE0 = 12
 TAIL = 256
 
-SCALE_LOADS = [(0, 16, 12), (12, 0, 32), (44, 4, 24), (68, 0, 32), (100, 4, 28)]
+QUANT_PIECES = [(0, 128), (128, 128), (256, 256)]
+PIECES = [[512, 512], [1024], [1024], [512, 256, 256]]
+SCALE_LOADS = [(12, 0, 32), (44, 4, 16), (60, 20, 8), (68, 0, 32), (108, 12, 4), (0, 16, 4)]
 
 
 def tile_list_tabres_none_kernel(
@@ -33,91 +35,92 @@ def tile_list_tabres_none_kernel(
         keep = ctx.enter_context(tc.tile_pool(name="keep", bufs=1))
         psum = ctx.enter_context(tc.psum_pool(name="psum", bufs=4))
 
+        half = M // 2
         offsets = keep.tile([P, S // 16], U16, name="offsets")
         scales = keep.tile([P, T // 4], I32, name="scales")
-        w8_raw = keep.tile([P, PACK, M], F32, name="w8_raw")
+        w8_raw = [keep.tile([P, PACK, half], F32, name=f"w8_raw{u}") for u in range(2)]
         words = [keep.tile([P, T], I32, name=f"words{a}") for a in range(2)]
         w4_codes = keep.tile([P, 2 * M], U8, name="w4_codes", align_bytes=64)
         w4_plane = keep.tile([P, M // 4], I32, name="w4_plane", align_bytes=64)
         resid = [keep.tile([P, T], F32, name=f"resid{m}") for m in range(ROW_TILES)]
 
+        nc.vector.memset(scales[96:P, :], 0)
+        nc.gpsimd.memset(scales[0:12, :], 0)
         nc.gpsimd.memset(w4_plane[:], 0)
         warm = keep.tile([P, 2], F32, name="warm")
         nc.vector.memset(warm[:, 0:1], 0.0)
-        nc.scalar.copy(warm[:, 1:2], warm[:, 0:1])
 
         table_words = [tab_words[a].rearrange("p t i -> p (t i)").bitcast(I32) for a in range(2)]
         scale_rows = tab_scales.rearrange("a q t -> (a q) t").bitcast(I32)
         w4_rows = w4_scales[0].bitcast(I32)
-        nc.sync.dma_start(words[1][:], table_words[1])
+        w8_rows = w8.rearrange("(p j) n -> p j n", j=PACK)
         nc.sync.dma_start(offsets[:], offs)
         for part, row, count in SCALE_LOADS:
-            queue = nc.scalar if part == 0 else nc.sync
-            queue.dma_start(scales[part : part + count, :], scale_rows[row : row + count, :])
+            nc.sync.dma_start(scales[part : part + count, :], scale_rows[row : row + count, :])
+        nc.scalar.copy(warm[:, 1:2], warm[:, 0:1])
+        nc.sync.dma_start(words[1][:], table_words[1])
         nc.sync.dma_start(words[0][:], table_words[0])
-        nc.sync.dma_start(w8_raw[:], w8.rearrange("(p j) n -> p j n", j=PACK))
         nc.sync.dma_start(w4_codes[:].bitcast(I32), w4_words[0].bitcast(I32))
         for q in range(4):
             nc.sync.dma_start(w4_plane[32 * q : 32 * q + 4, :], w4_rows[4 * q : 4 * q + 4, :])
-        for m in range(ROW_TILES):
+        for u in range(2):
+            nc.sync.dma_start(w8_raw[u][:], w8_rows[:, :, u * half : (u + 1) * half])
+            nc.sync.dma_start(resid[u][:], rT[u * P : (u + 1) * P, :])
+        for m in range(2, ROW_TILES):
             nc.sync.dma_start(resid[m][:], rT[m * P : (m + 1) * P, :])
 
         picked_scales = keep.tile([P, S], U8, name="picked_scales", align_bytes=64)
         picked_words = [keep.tile([P, S], U32, name=f"picked_words{a}", align_bytes=64) for a in range(2)]
-        nc.vector.tensor_copy(picked_words[1][:], words[1][:].bitcast(U32).indirect(offsets[:]))
         nc.vector.tensor_copy(picked_scales[:], scales[:].bitcast(U8).indirect(offsets[:]))
+        nc.vector.tensor_copy(picked_words[1][:], words[1][:].bitcast(U32).indirect(offsets[:]))
         nc.vector.tensor_copy(picked_words[0][:], words[0][:].bitcast(U32).indirect(offsets[:]))
 
-        half = M // 2
-        grouped = [keep.tile([P, half, PACK], BF16, name=f"grouped{u}", align_bytes=64) for u in range(2)]
         w8_codes = keep.tile([P, M], U32, name="w8_codes", align_bytes=64)
         w8_plane = keep.tile([P, M], U8, name="w8_plane", align_bytes=64)
-        for u in range(2):
-            cols = slice(u * half, (u + 1) * half)
+        for n0, width in QUANT_PIECES:
+            grouped = keep.tile([P, width, PACK], BF16, name=f"grouped{n0}", align_bytes=64)
+            raw = w8_raw[n0 // half][:, :, n0 % half : n0 % half + width]
             nc.scalar.copy(
-                grouped[u][:].rearrange("p (c i) t -> p c t i", i=4),
-                w8_raw[:, :, cols].rearrange("p t (c i) -> p c t i", i=4),
+                grouped[:].rearrange("p (c i) t -> p c t i", i=4),
+                raw.rearrange("p t (c i) -> p c t i", i=4),
             )
             nc.vector.quantize_mx(
-                out=w8_codes[:, cols].bitcast(FP8X4),
-                scales=w8_plane[:, cols],
-                in_=grouped[u][:].rearrange("p c t -> p (c t)"),
+                out=w8_codes[:, n0 : n0 + width].bitcast(FP8X4),
+                scales=w8_plane[:, n0 : n0 + width],
+                in_=grouped[:].rearrange("p c t -> p (c t)"),
             )
 
-        banks = {}
         for m in range(ROW_TILES):
             rows = slice(m * P, (m + 1) * P)
+            y_sb = keep.tile([P, S], F32, name=f"y_sb{m}")
             for h in range(S // N_TILE):
                 cols = slice(h * N_TILE, (h + 1) * N_TILE)
-                banks[m, h] = psum.tile([P, N_TILE], F32, name=f"acc{m}_{h}", tag="acc")
+                bank = psum.tile([P, N_TILE], F32, name=f"acc{m}_{h}", tag="acc")
                 nc.tensor.matmul_mx(
-                    out=banks[m, h][:],
+                    out=bank[:],
                     lhsT=w4_codes[:, 2 * m * P : 2 * (m + 1) * P].bitcast(FP4X4),
-                    lhsT_scale=w4_plane[:].bitcast(U8)[:, m * P : (m + 1) * P],
+                    lhsT_scale=w4_plane[:].bitcast(U8)[:, rows],
                     rhs=picked_words[1][:, cols].bitcast(FP8X4),
                     rhs_scale=picked_scales[:, cols],
                     start=True,
                     stop=False,
                 )
                 nc.tensor.matmul_mx(
-                    out=banks[m, h][:],
-                    lhsT=w8_codes[:, m * P : (m + 1) * P].bitcast(FP8X4),
-                    lhsT_scale=w8_plane[:, m * P : (m + 1) * P],
+                    out=bank[:],
+                    lhsT=w8_codes[:, rows].bitcast(FP8X4),
+                    lhsT_scale=w8_plane[:, rows],
                     rhs=picked_words[0][:, cols].bitcast(FP8X4),
                     rhs_scale=picked_scales[PLANE0:P, cols],
                     start=False,
                     stop=True,
                 )
+                nc.scalar.copy(y_sb[:, cols], bank[:])
 
-            for h in range(S // N_TILE):
-                c0 = h * N_TILE
-                y_sb = keep.tile([P, N_TILE], F32, name=f"y_sb{m}_{h}")
-                nc.scalar.copy(y_sb[:], banks[m, h][:])
-                last = (m, h) == (ROW_TILES - 1, S // N_TILE - 1)
-                width = TAIL if last else N_TILE
-                for b0 in range(0, N_TILE, width):
-                    result = keep.tile([P, width], F32, name=f"result{m}_{h}_{b0}")
-                    picks = offsets[:, (c0 + b0) // 16 : (c0 + b0 + width) // 16]
-                    nc.vector.tensor_tensor(result[:], resid[m][:].indirect(picks), y_sb[:, b0 : b0 + width], ADD)
-                    queue = nc.scalar if last else nc.sync
-                    queue.dma_start(out[rows, c0 + b0 : c0 + b0 + width], result[:])
+            c0 = 0
+            for width in PIECES[m]:
+                result = keep.tile([P, width], F32, name=f"result{m}_{c0}")
+                piece = offsets[:, c0 // 16 : (c0 + width) // 16]
+                nc.vector.tensor_tensor(result[:], resid[m][:].indirect(piece), y_sb[:, c0 : c0 + width], ADD)
+                queue = nc.scalar if width == TAIL else nc.sync
+                queue.dma_start(out[rows, c0 : c0 + width], result[:])
+                c0 = c0 + width

@@ -22,7 +22,6 @@ ROW_TILES = M // P
 PLANE0 = 12
 TAIL = 256
 
-QUANT_PIECES = [(0, 128), (128, 128), (256, 256)]
 PIECES = [[512, 512], [1024], [1024], [512, 256, 256]]
 SCALE_LOADS = [(12, 0, 32), (44, 4, 16), (60, 20, 8), (68, 0, 32), (108, 12, 4), (0, 16, 4)]
 
@@ -33,12 +32,12 @@ def tile_list_tabres_none_kernel(
     nc = tc.nc
     with ExitStack() as ctx:
         keep = ctx.enter_context(tc.tile_pool(name="keep", bufs=1))
-        psum = ctx.enter_context(tc.psum_pool(name="psum", bufs=4))
+        psum = ctx.enter_context(tc.psum_pool(name="psum", bufs=3))
 
         half = M // 2
         offsets = keep.tile([P, S // 16], U16, name="offsets")
         scales = keep.tile([P, T // 4], I32, name="scales")
-        w8_raw = [keep.tile([P, PACK, half], F32, name=f"w8_raw{u}") for u in range(2)]
+        w8_raw = keep.tile([P, PACK, M], F32, name="w8_raw")
         words = [keep.tile([P, T], I32, name=f"words{a}") for a in range(2)]
         w4_codes = keep.tile([P, 2 * M], U8, name="w4_codes", align_bytes=64)
         w4_plane = keep.tile([P, M // 4], I32, name="w4_plane", align_bytes=64)
@@ -46,7 +45,7 @@ def tile_list_tabres_none_kernel(
 
         nc.vector.memset(scales[96:P, :], 0)
         nc.gpsimd.memset(scales[0:12, :], 0)
-        nc.gpsimd.memset(w4_plane[:], 0)
+        nc.vector.memset(w4_plane[:], 0)
         warm = keep.tile([P, 2], F32, name="warm")
         nc.vector.memset(warm[:, 0:1], 0.0)
 
@@ -58,37 +57,39 @@ def tile_list_tabres_none_kernel(
         for part, row, count in SCALE_LOADS:
             nc.sync.dma_start(scales[part : part + count, :], scale_rows[row : row + count, :])
         nc.scalar.copy(warm[:, 1:2], warm[:, 0:1])
-        nc.sync.dma_start(words[1][:], table_words[1])
         nc.sync.dma_start(words[0][:], table_words[0])
+        nc.sync.dma_start(w8_raw[:], w8_rows)
+        nc.sync.dma_start(words[1][:], table_words[1])
         nc.sync.dma_start(w4_codes[:].bitcast(I32), w4_words[0].bitcast(I32))
         for q in range(4):
             nc.sync.dma_start(w4_plane[32 * q : 32 * q + 4, :], w4_rows[4 * q : 4 * q + 4, :])
-        for u in range(2):
-            nc.sync.dma_start(w8_raw[u][:], w8_rows[:, :, u * half : (u + 1) * half])
-            nc.sync.dma_start(resid[u][:], rT[u * P : (u + 1) * P, :])
-        for m in range(2, ROW_TILES):
+        for m in range(ROW_TILES):
             nc.sync.dma_start(resid[m][:], rT[m * P : (m + 1) * P, :])
 
         picked_scales = keep.tile([P, S], U8, name="picked_scales", align_bytes=64)
-        picked_words = [keep.tile([P, S], U32, name=f"picked_words{a}", align_bytes=64) for a in range(2)]
+        picked_words0 = keep.tile([P, S], U32, name="picked_words0", align_bytes=64)
+        picked_words1 = [keep.tile([P, N_TILE], U32, name=f"picked_words1_{h}", align_bytes=64) for h in range(2)]
         nc.vector.tensor_copy(picked_scales[:], scales[:].bitcast(U8).indirect(offsets[:]))
-        nc.vector.tensor_copy(picked_words[1][:], words[1][:].bitcast(U32).indirect(offsets[:]))
-        nc.vector.tensor_copy(picked_words[0][:], words[0][:].bitcast(U32).indirect(offsets[:]))
+        nc.vector.tensor_copy(picked_words0[:], words[0][:].bitcast(U32).indirect(offsets[:]))
 
         w8_codes = keep.tile([P, M], U32, name="w8_codes", align_bytes=64)
         w8_plane = keep.tile([P, M], U8, name="w8_plane", align_bytes=64)
-        for n0, width in QUANT_PIECES:
-            grouped = keep.tile([P, width, PACK], BF16, name=f"grouped{n0}", align_bytes=64)
-            raw = w8_raw[n0 // half][:, :, n0 % half : n0 % half + width]
-            nc.scalar.copy(
+        for u, interleave in enumerate((nc.scalar.copy, nc.vector.tensor_copy)):
+            cols = slice(u * half, (u + 1) * half)
+            grouped = keep.tile([P, half, PACK], BF16, name=f"grouped{u}", align_bytes=64)
+            interleave(
                 grouped[:].rearrange("p (c i) t -> p c t i", i=4),
-                raw.rearrange("p t (c i) -> p c t i", i=4),
+                w8_raw[:, :, cols].rearrange("p t (c i) -> p c t i", i=4),
             )
             nc.vector.quantize_mx(
-                out=w8_codes[:, n0 : n0 + width].bitcast(FP8X4),
-                scales=w8_plane[:, n0 : n0 + width],
+                out=w8_codes[:, cols].bitcast(FP8X4),
+                scales=w8_plane[:, cols],
                 in_=grouped[:].rearrange("p c t -> p (c t)"),
             )
+
+        for h in range(2):
+            picks = offsets[:, h * N_TILE // 16 : (h + 1) * N_TILE // 16]
+            nc.vector.tensor_copy(picked_words1[h][:], words[1][:].bitcast(U32).indirect(picks))
 
         for m in range(ROW_TILES):
             rows = slice(m * P, (m + 1) * P)
@@ -98,19 +99,19 @@ def tile_list_tabres_none_kernel(
                 bank = psum.tile([P, N_TILE], F32, name=f"acc{m}_{h}", tag="acc")
                 nc.tensor.matmul_mx(
                     out=bank[:],
-                    lhsT=w4_codes[:, 2 * m * P : 2 * (m + 1) * P].bitcast(FP4X4),
-                    lhsT_scale=w4_plane[:].bitcast(U8)[:, rows],
-                    rhs=picked_words[1][:, cols].bitcast(FP8X4),
-                    rhs_scale=picked_scales[:, cols],
+                    lhsT=w8_codes[:, rows].bitcast(FP8X4),
+                    lhsT_scale=w8_plane[:, rows],
+                    rhs=picked_words0[:, cols].bitcast(FP8X4),
+                    rhs_scale=picked_scales[PLANE0:P, cols],
                     start=True,
                     stop=False,
                 )
                 nc.tensor.matmul_mx(
                     out=bank[:],
-                    lhsT=w8_codes[:, rows].bitcast(FP8X4),
-                    lhsT_scale=w8_plane[:, rows],
-                    rhs=picked_words[0][:, cols].bitcast(FP8X4),
-                    rhs_scale=picked_scales[PLANE0:P, cols],
+                    lhsT=w4_codes[:, 2 * m * P : 2 * (m + 1) * P].bitcast(FP4X4),
+                    lhsT_scale=w4_plane[:].bitcast(U8)[:, rows],
+                    rhs=picked_words1[h][:].bitcast(FP8X4),
+                    rhs_scale=picked_scales[:, cols],
                     start=False,
                     stop=True,
                 )

@@ -22,7 +22,7 @@ ROW_TILES = M // P
 PLANE0 = 12
 TAIL = 256
 
-PIECES = [[512, 512], [1024], [1024], [512, 256, 256]]
+PIECES = [[512, 512], [1024], [1024], [512, 384, 128]]
 SCALE_LOADS = [(12, 0, 32), (44, 4, 16), (60, 20, 8), (68, 0, 32), (108, 12, 4), (0, 16, 4)]
 
 
@@ -32,7 +32,7 @@ def tile_list_tabres_none_kernel(
     nc = tc.nc
     with ExitStack() as ctx:
         keep = ctx.enter_context(tc.tile_pool(name="keep", bufs=1))
-        psum = ctx.enter_context(tc.psum_pool(name="psum", bufs=3))
+        psum = ctx.enter_context(tc.psum_pool(name="psum", bufs=5))
 
         half = M // 2
         offsets = keep.tile([P, S // 16], U16, name="offsets")
@@ -55,28 +55,30 @@ def tile_list_tabres_none_kernel(
         w8_rows = w8.rearrange("(p j) n -> p j n", j=PACK)
         nc.sync.dma_start(offsets[:], offs)
         for part, row, count in SCALE_LOADS:
-            nc.sync.dma_start(scales[part : part + count, :], scale_rows[row : row + count, :])
+            queue = nc.scalar if part in (44, 60, 0) else nc.sync
+            queue.dma_start(scales[part : part + count, :], scale_rows[row : row + count, :])
         nc.scalar.copy(warm[:, 1:2], warm[:, 0:1])
-        nc.sync.dma_start(words[0][:], table_words[0])
-        nc.sync.dma_start(w8_raw[:], w8_rows)
         nc.sync.dma_start(words[1][:], table_words[1])
         nc.sync.dma_start(w4_codes[:].bitcast(I32), w4_words[0].bitcast(I32))
         for q in range(4):
             nc.sync.dma_start(w4_plane[32 * q : 32 * q + 4, :], w4_rows[4 * q : 4 * q + 4, :])
+        nc.sync.dma_start(words[0][:], table_words[0])
+        nc.sync.dma_start(w8_raw[:], w8_rows)
         for m in range(ROW_TILES):
             nc.sync.dma_start(resid[m][:], rT[m * P : (m + 1) * P, :])
 
         picked_scales = keep.tile([P, S], U8, name="picked_scales", align_bytes=64)
-        picked_words0 = keep.tile([P, S], U32, name="picked_words0", align_bytes=64)
-        picked_words1 = [keep.tile([P, N_TILE], U32, name=f"picked_words1_{h}", align_bytes=64) for h in range(2)]
+        picked_words = [keep.tile([P, S], U32, name=f"picked_words{a}", align_bytes=64) for a in range(2)]
         nc.vector.tensor_copy(picked_scales[:], scales[:].bitcast(U8).indirect(offsets[:]))
-        nc.vector.tensor_copy(picked_words0[:], words[0][:].bitcast(U32).indirect(offsets[:]))
+        for a in (1, 0):
+            nc.vector.tensor_copy(picked_words[a][:], words[a][:].bitcast(U32).indirect(offsets[:]))
 
         w8_codes = keep.tile([P, M], U32, name="w8_codes", align_bytes=64)
         w8_plane = keep.tile([P, M], U8, name="w8_plane", align_bytes=64)
-        for u, interleave in enumerate((nc.scalar.copy, nc.vector.tensor_copy)):
-            cols = slice(u * half, (u + 1) * half)
-            grouped = keep.tile([P, half, PACK], BF16, name=f"grouped{u}", align_bytes=64)
+        pieces = [(0, P, nc.vector.tensor_copy), (P, P, nc.vector.tensor_copy), (half, half, nc.scalar.copy)]
+        for n0, width, interleave in pieces:
+            cols = slice(n0, n0 + width)
+            grouped = keep.tile([P, width, PACK], BF16, name=f"grouped{n0}", align_bytes=64)
             interleave(
                 grouped[:].rearrange("p (c i) t -> p c t i", i=4),
                 w8_raw[:, :, cols].rearrange("p t (c i) -> p c t i", i=4),
@@ -87,41 +89,39 @@ def tile_list_tabres_none_kernel(
                 in_=grouped[:].rearrange("p c t -> p (c t)"),
             )
 
-        for h in range(2):
-            picks = offsets[:, h * N_TILE // 16 : (h + 1) * N_TILE // 16]
-            nc.vector.tensor_copy(picked_words1[h][:], words[1][:].bitcast(U32).indirect(picks))
-
         for m in range(ROW_TILES):
             rows = slice(m * P, (m + 1) * P)
-            y_sb = keep.tile([P, S], F32, name=f"y_sb{m}")
+            span = max(N_TILE, PIECES[m][0])
+            y_sb = [keep.tile([P, span], F32, name=f"y_sb{m}_{t}") for t in range(S // span)]
             for h in range(S // N_TILE):
                 cols = slice(h * N_TILE, (h + 1) * N_TILE)
                 bank = psum.tile([P, N_TILE], F32, name=f"acc{m}_{h}", tag="acc")
                 nc.tensor.matmul_mx(
                     out=bank[:],
-                    lhsT=w8_codes[:, rows].bitcast(FP8X4),
-                    lhsT_scale=w8_plane[:, rows],
-                    rhs=picked_words0[:, cols].bitcast(FP8X4),
-                    rhs_scale=picked_scales[PLANE0:P, cols],
+                    lhsT=w4_codes[:, 2 * m * P : 2 * (m + 1) * P].bitcast(FP4X4),
+                    lhsT_scale=w4_plane[:].bitcast(U8)[:, rows],
+                    rhs=picked_words[1][:, cols].bitcast(FP8X4),
+                    rhs_scale=picked_scales[:, cols],
                     start=True,
                     stop=False,
                 )
                 nc.tensor.matmul_mx(
                     out=bank[:],
-                    lhsT=w4_codes[:, 2 * m * P : 2 * (m + 1) * P].bitcast(FP4X4),
-                    lhsT_scale=w4_plane[:].bitcast(U8)[:, rows],
-                    rhs=picked_words1[h][:].bitcast(FP8X4),
-                    rhs_scale=picked_scales[:, cols],
+                    lhsT=w8_codes[:, rows].bitcast(FP8X4),
+                    lhsT_scale=w8_plane[:, rows],
+                    rhs=picked_words[0][:, cols].bitcast(FP8X4),
+                    rhs_scale=picked_scales[PLANE0:P, cols],
                     start=False,
                     stop=True,
                 )
-                nc.scalar.copy(y_sb[:, cols], bank[:])
+                y0 = h * N_TILE % span
+                nc.scalar.copy(y_sb[h * N_TILE // span][:, y0 : y0 + N_TILE], bank[:])
 
             c0 = 0
             for width in PIECES[m]:
                 result = keep.tile([P, width], F32, name=f"result{m}_{c0}")
                 piece = offsets[:, c0 // 16 : (c0 + width) // 16]
-                nc.vector.tensor_tensor(result[:], resid[m][:].indirect(piece), y_sb[:, c0 : c0 + width], ADD)
-                queue = nc.scalar if width == TAIL else nc.sync
+                nc.vector.tensor_tensor(result[:], resid[m][:].indirect(piece), y_sb[c0 // span][:, c0 % span : c0 % span + width], ADD)
+                queue = nc.scalar if width < N_TILE else nc.sync
                 queue.dma_start(out[rows, c0 : c0 + width], result[:])
                 c0 = c0 + width

@@ -89,6 +89,7 @@ def tile_list_tabres_none_kernel(
                 in_=grouped[:].rearrange("p c t -> p (c t)"),
             )
 
+        early = keep.tile([P, 2, S], F32, name="early")
         for m in range(ROW_TILES):
             rows = slice(m * P, (m + 1) * P)
             span = max(N_TILE, PIECES[m][0])
@@ -118,10 +119,17 @@ def tile_list_tabres_none_kernel(
                 nc.scalar.copy(y_sb[h * N_TILE // span][:, y0 : y0 + N_TILE], bank[:])
 
             c0 = 0
-            for width in PIECES[m]:
-                result = keep.tile([P, width], F32, name=f"result{m}_{c0}")
+            for t, width in enumerate(PIECES[m]):
+                if m < 2:
+                    result = early[:, m, c0 : c0 + width]
+                else:
+                    late = keep.tile([P, width], F32, name=f"result{m}_{c0}")
+                    result = late[:]
                 piece = offsets[:, c0 // 16 : (c0 + width) // 16]
-                nc.vector.tensor_tensor(result[:], resid[m][:].indirect(piece), y_sb[c0 // span][:, c0 % span : c0 % span + width], ADD)
-                queue = nc.scalar if width < N_TILE else nc.sync
-                queue.dma_start(out[rows, c0 : c0 + width], result[:])
+                nc.vector.tensor_tensor(result, resid[m][:].indirect(piece), y_sb[c0 // span][:, c0 % span : c0 % span + width], ADD)
+                if m >= 2:
+                    queue = nc.scalar if (m + t) % 2 == 0 else nc.sync
+                    queue.dma_start(out[rows, c0 : c0 + width], result)
                 c0 = c0 + width
+            if m == 1:
+                nc.sync.dma_start(out[0 : 2 * P, :].rearrange("(m p) j -> p m j", p=P), early[:])

@@ -32,7 +32,7 @@ def tile_list_tabres_none_kernel(
     nc = tc.nc
     with ExitStack() as ctx:
         keep = ctx.enter_context(tc.tile_pool(name="keep", bufs=1))
-        psum = ctx.enter_context(tc.psum_pool(name="psum", bufs=5))
+        psum = ctx.enter_context(tc.psum_pool(name="psum", bufs=4))
 
         half = M // 2
         offsets = keep.tile([P, S // 16], U16, name="offsets")
@@ -46,8 +46,6 @@ def tile_list_tabres_none_kernel(
         nc.vector.memset(scales[96:P, :], 0)
         nc.gpsimd.memset(scales[0:12, :], 0)
         nc.vector.memset(w4_plane[:], 0)
-        warm = keep.tile([P, 2], F32, name="warm")
-        nc.vector.memset(warm[:, 0:1], 0.0)
 
         table_words = [tab_words[a].rearrange("p t i -> p (t i)").bitcast(I32) for a in range(2)]
         scale_rows = tab_scales.rearrange("a q t -> (a q) t").bitcast(I32)
@@ -57,12 +55,11 @@ def tile_list_tabres_none_kernel(
         for part, row, count in SCALE_LOADS:
             queue = nc.scalar if part in (44, 60, 0) else nc.sync
             queue.dma_start(scales[part : part + count, :], scale_rows[row : row + count, :])
-        nc.scalar.copy(warm[:, 1:2], warm[:, 0:1])
         nc.sync.dma_start(words[1][:], table_words[1])
+        nc.sync.dma_start(words[0][:], table_words[0])
         nc.sync.dma_start(w4_codes[:].bitcast(I32), w4_words[0].bitcast(I32))
         for q in range(4):
             nc.sync.dma_start(w4_plane[32 * q : 32 * q + 4, :], w4_rows[4 * q : 4 * q + 4, :])
-        nc.sync.dma_start(words[0][:], table_words[0])
         nc.sync.dma_start(w8_raw[:], w8_rows)
         for m in range(ROW_TILES):
             nc.sync.dma_start(resid[m][:], rT[m * P : (m + 1) * P, :])

@@ -20,9 +20,9 @@ PACK = 4
 N_TILE = 512
 ROW_TILES = M // P
 PLANE0 = 12
-TAIL = 256
 
-PIECES = [[512, 512], [1024], [1024], [512, 384, 128]]
+BANKS = [[256, 256, 512], [512, 512], [512, 512], [512, 512]]
+PIECES = [[256, 256, 512], [1024], [1024], [512, 384, 128]]
 SCALE_LOADS = [(12, 0, 32), (44, 4, 16), (60, 20, 8), (68, 0, 32), (108, 12, 4), (0, 16, 4)]
 
 
@@ -89,22 +89,31 @@ def tile_list_tabres_none_kernel(
         early = keep.tile([P, 2, S], F32, name="early")
         for m in range(ROW_TILES):
             rows = slice(m * P, (m + 1) * P)
-            span = max(N_TILE, PIECES[m][0])
-            y_sb = [keep.tile([P, span], F32, name=f"y_sb{m}_{t}") for t in range(S // span)]
-            for h in range(S // N_TILE):
-                cols = slice(h * N_TILE, (h + 1) * N_TILE)
+            spans = [S] if PIECES[m][0] == S else BANKS[m]
+            starts = [sum(spans[:t]) for t in range(len(spans))]
+            y_sb = [keep.tile([P, span], F32, name=f"y_sb{m}_{t}") for t, span in enumerate(spans)]
+
+            def sums_at(c0, width):
+                t = max(i for i, start in enumerate(starts) if start <= c0)
+                return y_sb[t][:, c0 - starts[t] : c0 - starts[t] + width]
+
+            b0 = 0
+            for h, wide in enumerate(BANKS[m]):
+                cols = slice(b0, b0 + wide)
                 bank = psum.tile([P, N_TILE], F32, name=f"acc{m}_{h}", tag="acc")
+                step = N_TILE if wide == N_TILE else P
+                for o in range(0, wide, step):
+                    nc.tensor.matmul_mx(
+                        out=bank[:, o : o + step],
+                        lhsT=w4_codes[:, 2 * m * P : 2 * (m + 1) * P].bitcast(FP4X4),
+                        lhsT_scale=w4_plane[:].bitcast(U8)[:, rows],
+                        rhs=picked_words[1][:, b0 + o : b0 + o + step].bitcast(FP8X4),
+                        rhs_scale=picked_scales[:, b0 + o : b0 + o + step],
+                        start=o == 0,
+                        stop=False,
+                    )
                 nc.tensor.matmul_mx(
-                    out=bank[:],
-                    lhsT=w4_codes[:, 2 * m * P : 2 * (m + 1) * P].bitcast(FP4X4),
-                    lhsT_scale=w4_plane[:].bitcast(U8)[:, rows],
-                    rhs=picked_words[1][:, cols].bitcast(FP8X4),
-                    rhs_scale=picked_scales[:, cols],
-                    start=True,
-                    stop=False,
-                )
-                nc.tensor.matmul_mx(
-                    out=bank[:],
+                    out=bank[:, 0:wide],
                     lhsT=w8_codes[:, rows].bitcast(FP8X4),
                     lhsT_scale=w8_plane[:, rows],
                     rhs=picked_words[0][:, cols].bitcast(FP8X4),
@@ -112,8 +121,8 @@ def tile_list_tabres_none_kernel(
                     start=False,
                     stop=True,
                 )
-                y0 = h * N_TILE % span
-                nc.scalar.copy(y_sb[h * N_TILE // span][:, y0 : y0 + N_TILE], bank[:])
+                nc.scalar.copy(sums_at(b0, wide), bank[:, 0:wide])
+                b0 = b0 + wide
 
             c0 = 0
             for t, width in enumerate(PIECES[m]):
@@ -123,7 +132,7 @@ def tile_list_tabres_none_kernel(
                     late = keep.tile([P, width], F32, name=f"result{m}_{c0}")
                     result = late[:]
                 piece = offsets[:, c0 // 16 : (c0 + width) // 16]
-                nc.vector.tensor_tensor(result, resid[m][:].indirect(piece), y_sb[c0 // span][:, c0 % span : c0 % span + width], ADD)
+                nc.vector.tensor_tensor(result, resid[m][:].indirect(piece), sums_at(c0, width), ADD)
                 if m >= 2:
                     queue = nc.scalar if (m + t) % 2 == 0 else nc.sync
                     queue.dma_start(out[rows, c0 : c0 + width], result)

@@ -44,7 +44,7 @@ def tile_list_tabres_none_kernel(
         resid = [keep.tile([P, T], F32, name=f"resid{m}") for m in range(ROW_TILES)]
 
         nc.vector.memset(scales[96:P, :], 0)
-        nc.gpsimd.memset(scales[0:12, :], 0)
+        nc.vector.memset(scales[0:12, :], 0)
         nc.vector.memset(w4_plane[:], 0)
 
         table_words = [tab_words[a].rearrange("p t i -> p (t i)").bitcast(I32) for a in range(2)]
@@ -53,7 +53,7 @@ def tile_list_tabres_none_kernel(
         w8_rows = w8.rearrange("(p j) n -> p j n", j=PACK)
         nc.sync.dma_start(offsets[:], offs)
         for part, row, count in SCALE_LOADS:
-            queue = nc.scalar if part in (44, 60, 0) else nc.sync
+            queue = nc.scalar if part in (44, 60) else nc.sync
             queue.dma_start(scales[part : part + count, :], scale_rows[row : row + count, :])
         nc.sync.dma_start(words[1][:], table_words[1])
         nc.sync.dma_start(words[0][:], table_words[0])

@@ -16,26 +16,39 @@ FP4X4 = mybir.dt.float4_e2m1fn_x4
 ADD = mybir.AluOpType.add
 
 P = 128
+QUADRANT = 32
 PACK = 4
-N_TILE = 512
+GROUP = 16
+BANK = 512
 ROW_TILES = M // P
+JOINT_TILES = 2
+
 PLANE0 = 12
 
-BANKS = [[256, 256, 512], [512, 512], [512, 512], [512, 512]]
-PIECES = [[256, 256, 512], [1024], [1024], [512, 384, 128]]
-SCALE_LOADS = [(12, 0, 32), (44, 4, 16), (60, 20, 8), (68, 0, 32), (108, 12, 4), (0, 16, 4)]
+SCALE_LOADS = [
+    ("sync", PLANE0, 0, 32),
+    ("scalar", PLANE0 + QUADRANT, 4, 16),
+    ("scalar", PLANE0 + QUADRANT + 16, 4 + 16, 8),
+    ("sync", PLANE0 + 2 * QUADRANT - 8, 0, 32),
+    ("sync", PLANE0 + 3 * QUADRANT, 12, PACK),
+    ("sync", 0, 16, PACK),
+]
+
+GROUP_WIDTHS = [[256, 256, 512], [512, 512], [512, 512], [512, 512]]
+ADD_WIDTHS = [[256, 256, 512], [1024], [1024], [512, 384, 128]]
+OPEN_BANKS = 4
 
 
 def tile_list_tabres_none_kernel(
     tc, tab_words, tab_scales, w8, w4_words, w4_scales, rT, offs, out
 ):
     nc = tc.nc
+    queues = {"sync": nc.sync, "scalar": nc.scalar}
     with ExitStack() as ctx:
         keep = ctx.enter_context(tc.tile_pool(name="keep", bufs=1))
-        psum = ctx.enter_context(tc.psum_pool(name="psum", bufs=4))
+        psum = ctx.enter_context(tc.psum_pool(name="psum", bufs=OPEN_BANKS))
 
-        half = M // 2
-        offsets = keep.tile([P, S // 16], U16, name="offsets")
+        offsets = keep.tile([P, S // GROUP], U16, name="offsets")
         scales = keep.tile([P, T // 4], I32, name="scales")
         w8_raw = keep.tile([P, PACK, M], F32, name="w8_raw")
         words = [keep.tile([P, T], I32, name=f"words{a}") for a in range(2)]
@@ -43,23 +56,23 @@ def tile_list_tabres_none_kernel(
         w4_plane = keep.tile([P, M // 4], I32, name="w4_plane", align_bytes=64)
         resid = [keep.tile([P, T], F32, name=f"resid{m}") for m in range(ROW_TILES)]
 
-        nc.vector.memset(scales[96:P, :], 0)
-        nc.vector.memset(scales[0:12, :], 0)
-        nc.vector.memset(w4_plane[:], 0)
+        nc.vector.memset(scales[3 * QUADRANT : P, :], 0)
+        nc.vector.memset(scales[0:PLANE0, :], 0)
 
         table_words = [tab_words[a].rearrange("p t i -> p (t i)").bitcast(I32) for a in range(2)]
         scale_rows = tab_scales.rearrange("a q t -> (a q) t").bitcast(I32)
         w4_rows = w4_scales[0].bitcast(I32)
         w8_rows = w8.rearrange("(p j) n -> p j n", j=PACK)
         nc.sync.dma_start(offsets[:], offs)
-        for part, row, count in SCALE_LOADS:
-            queue = nc.scalar if part in (44, 60) else nc.sync
-            queue.dma_start(scales[part : part + count, :], scale_rows[row : row + count, :])
+        for queue, part, row, count in SCALE_LOADS:
+            queues[queue].dma_start(scales[part : part + count, :], scale_rows[row : row + count, :])
         nc.sync.dma_start(words[1][:], table_words[1])
         nc.sync.dma_start(words[0][:], table_words[0])
         nc.sync.dma_start(w4_codes[:].bitcast(I32), w4_words[0].bitcast(I32))
-        for q in range(4):
-            nc.sync.dma_start(w4_plane[32 * q : 32 * q + 4, :], w4_rows[4 * q : 4 * q + 4, :])
+        for q in range(P // QUADRANT):
+            nc.sync.dma_start(
+                w4_plane[QUADRANT * q : QUADRANT * q + PACK, :], w4_rows[PACK * q : PACK * (q + 1), :]
+            )
         nc.sync.dma_start(w8_raw[:], w8_rows)
         for m in range(ROW_TILES):
             nc.sync.dma_start(resid[m][:], rT[m * P : (m + 1) * P, :])
@@ -72,43 +85,43 @@ def tile_list_tabres_none_kernel(
 
         w8_codes = keep.tile([P, M], U32, name="w8_codes", align_bytes=64)
         w8_plane = keep.tile([P, M], U8, name="w8_plane", align_bytes=64)
-        pieces = [(0, P, nc.vector.tensor_copy), (P, P, nc.vector.tensor_copy), (half, half, nc.scalar.copy)]
-        for n0, width, interleave in pieces:
-            cols = slice(n0, n0 + width)
-            grouped = keep.tile([P, width, PACK], BF16, name=f"grouped{n0}", align_bytes=64)
+        shares = [(0, P, nc.vector.tensor_copy), (P, P, nc.vector.tensor_copy), (2 * P, 2 * P, nc.scalar.copy)]
+        for n0, count, interleave in shares:
+            channels = slice(n0, n0 + count)
+            grouped = keep.tile([P, count, PACK], BF16, name=f"grouped{n0}", align_bytes=64)
             interleave(
                 grouped[:].rearrange("p (c i) t -> p c t i", i=4),
-                w8_raw[:, :, cols].rearrange("p t (c i) -> p c t i", i=4),
+                w8_raw[:, :, channels].rearrange("p t (c i) -> p c t i", i=4),
             )
             nc.vector.quantize_mx(
-                out=w8_codes[:, cols].bitcast(FP8X4),
-                scales=w8_plane[:, cols],
+                out=w8_codes[:, channels].bitcast(FP8X4),
+                scales=w8_plane[:, channels],
                 in_=grouped[:].rearrange("p c t -> p (c t)"),
             )
 
-        early = keep.tile([P, 2, S], F32, name="early")
+        joint = keep.tile([P, JOINT_TILES, S], F32, name="joint")
         for m in range(ROW_TILES):
             rows = slice(m * P, (m + 1) * P)
-            spans = [S] if PIECES[m][0] == S else BANKS[m]
-            starts = [sum(spans[:t]) for t in range(len(spans))]
-            y_sb = [keep.tile([P, span], F32, name=f"y_sb{m}_{t}") for t, span in enumerate(spans)]
 
-            def sums_at(c0, width):
-                t = max(i for i, start in enumerate(starts) if start <= c0)
-                return y_sb[t][:, c0 - starts[t] : c0 - starts[t] + width]
+            spans = [S] if ADD_WIDTHS[m] == [S] else GROUP_WIDTHS[m]
+            starts = [sum(spans[:i]) for i in range(len(spans))]
+            sums = [keep.tile([P, span], F32, name=f"sums{m}_{i}") for i, span in enumerate(spans)]
 
-            b0 = 0
-            for h, wide in enumerate(BANKS[m]):
-                cols = slice(b0, b0 + wide)
-                bank = psum.tile([P, N_TILE], F32, name=f"acc{m}_{h}", tag="acc")
-                step = N_TILE if wide == N_TILE else P
+            def sums_at(first, width):
+                i = max(i for i, start in enumerate(starts) if start <= first)
+                return sums[i][:, first - starts[i] : first - starts[i] + width]
+
+            g0 = 0
+            for h, wide in enumerate(GROUP_WIDTHS[m]):
+                bank = psum.tile([P, BANK], F32, name=f"acc{m}_{h}", tag="acc")
+                step = BANK if wide == BANK else P
                 for o in range(0, wide, step):
                     nc.tensor.matmul_mx(
                         out=bank[:, o : o + step],
                         lhsT=w4_codes[:, 2 * m * P : 2 * (m + 1) * P].bitcast(FP4X4),
                         lhsT_scale=w4_plane[:].bitcast(U8)[:, rows],
-                        rhs=picked_words[1][:, b0 + o : b0 + o + step].bitcast(FP8X4),
-                        rhs_scale=picked_scales[:, b0 + o : b0 + o + step],
+                        rhs=picked_words[1][:, g0 + o : g0 + o + step].bitcast(FP8X4),
+                        rhs_scale=picked_scales[:, g0 + o : g0 + o + step],
                         start=o == 0,
                         stop=False,
                     )
@@ -116,26 +129,26 @@ def tile_list_tabres_none_kernel(
                     out=bank[:, 0:wide],
                     lhsT=w8_codes[:, rows].bitcast(FP8X4),
                     lhsT_scale=w8_plane[:, rows],
-                    rhs=picked_words[0][:, cols].bitcast(FP8X4),
-                    rhs_scale=picked_scales[PLANE0:P, cols],
+                    rhs=picked_words[0][:, g0 : g0 + wide].bitcast(FP8X4),
+                    rhs_scale=picked_scales[PLANE0:P, g0 : g0 + wide],
                     start=False,
                     stop=True,
                 )
-                nc.scalar.copy(sums_at(b0, wide), bank[:, 0:wide])
-                b0 = b0 + wide
+                nc.scalar.copy(sums_at(g0, wide), bank[:, 0:wide])
+                g0 = g0 + wide
 
             c0 = 0
-            for t, width in enumerate(PIECES[m]):
-                if m < 2:
-                    result = early[:, m, c0 : c0 + width]
+            for piece, width in enumerate(ADD_WIDTHS[m]):
+                if m < JOINT_TILES:
+                    result = joint[:, m, c0 : c0 + width]
                 else:
-                    late = keep.tile([P, width], F32, name=f"result{m}_{c0}")
-                    result = late[:]
-                piece = offsets[:, c0 // 16 : (c0 + width) // 16]
-                nc.vector.tensor_tensor(result, resid[m][:].indirect(piece), sums_at(c0, width), ADD)
-                if m >= 2:
-                    queue = nc.scalar if (m + t) % 2 == 0 else nc.sync
-                    queue.dma_start(out[rows, c0 : c0 + width], result)
+                    single = keep.tile([P, width], F32, name=f"result{m}_{c0}")
+                    result = single[:]
+                entries = offsets[:, c0 // GROUP : (c0 + width) // GROUP]
+                nc.vector.tensor_tensor(result, resid[m][:].indirect(entries), sums_at(c0, width), ADD)
+                if m >= JOINT_TILES:
+                    store_queue = nc.scalar if (m + piece) % 2 == 0 else nc.sync
+                    store_queue.dma_start(out[rows, c0 : c0 + width], result)
                 c0 = c0 + width
-            if m == 1:
-                nc.sync.dma_start(out[0 : 2 * P, :].rearrange("(m p) j -> p m j", p=P), early[:])
+            if m == JOINT_TILES - 1:
+                nc.sync.dma_start(out[0 : JOINT_TILES * P, :].rearrange("(m p) j -> p m j", p=P), joint[:])

@@ -69,10 +69,8 @@ def tile_list_tabres_none_kernel(
         nc.sync.dma_start(words[1][:], table_words[1])
         nc.sync.dma_start(words[0][:], table_words[0])
         nc.sync.dma_start(w4_codes[:].bitcast(I32), w4_words[0].bitcast(I32))
-        for q in range(P // QUADRANT):
-            nc.sync.dma_start(
-                w4_plane[QUADRANT * q : QUADRANT * q + PACK, :], w4_rows[PACK * q : PACK * (q + 1), :]
-            )
+        for r in range(PACK):
+            nc.sync.dma_start(w4_plane[r:P:QUADRANT, :], w4_rows[r : PACK * PACK : PACK, :])
         nc.sync.dma_start(w8_raw[:], w8_rows)
         for m in range(ROW_TILES):
             nc.sync.dma_start(resid[m][:], rT[m * P : (m + 1) * P, :])

@@ -20,6 +20,7 @@ QUADRANT = 32
 PACK = 4
 GROUP = 16
 BANK = 512
+DMA_ALIGN = 256
 ROW_TILES = M // P
 JOINT_TILES = 2
 
@@ -48,13 +49,13 @@ def tile_list_tabres_none_kernel(
         keep = ctx.enter_context(tc.tile_pool(name="keep", bufs=1))
         psum = ctx.enter_context(tc.psum_pool(name="psum", bufs=OPEN_BANKS))
 
-        offsets = keep.tile([P, S // GROUP], U16, name="offsets")
-        scales = keep.tile([P, T // 4], I32, name="scales")
-        w8_raw = keep.tile([P, PACK, M], F32, name="w8_raw")
-        words = [keep.tile([P, T], I32, name=f"words{a}") for a in range(2)]
-        w4_codes = keep.tile([P, 2 * M], U8, name="w4_codes", align_bytes=64)
-        w4_plane = keep.tile([P, M // 4], I32, name="w4_plane", align_bytes=64)
-        resid = [keep.tile([P, T], F32, name=f"resid{m}") for m in range(ROW_TILES)]
+        offsets = keep.tile([P, S // GROUP], U16, name="offsets", align_bytes=DMA_ALIGN)
+        scales = keep.tile([P, T // 4], I32, name="scales", align_bytes=DMA_ALIGN)
+        w8_raw = keep.tile([P, PACK, M], F32, name="w8_raw", align_bytes=DMA_ALIGN)
+        words = [keep.tile([P, T], I32, name=f"words{a}", align_bytes=DMA_ALIGN) for a in range(2)]
+        w4_codes = keep.tile([P, 2 * M], U8, name="w4_codes", align_bytes=DMA_ALIGN)
+        w4_plane = keep.tile([P, M // 4], I32, name="w4_plane", align_bytes=DMA_ALIGN)
+        resid = [keep.tile([P, T], F32, name=f"resid{m}", align_bytes=DMA_ALIGN) for m in range(ROW_TILES)]
 
         nc.vector.memset(scales[3 * QUADRANT : P, :], 0)
         nc.vector.memset(scales[0:PLANE0, :], 0)
@@ -97,7 +98,7 @@ def tile_list_tabres_none_kernel(
                 in_=grouped[:].rearrange("p c t -> p (c t)"),
             )
 
-        joint = keep.tile([P, JOINT_TILES, S], F32, name="joint")
+        joint = keep.tile([P, JOINT_TILES, S], F32, name="joint", align_bytes=DMA_ALIGN)
         for m in range(ROW_TILES):
             rows = slice(m * P, (m + 1) * P)
 
@@ -140,7 +141,7 @@ def tile_list_tabres_none_kernel(
                 if m < JOINT_TILES:
                     result = joint[:, m, c0 : c0 + width]
                 else:
-                    single = keep.tile([P, width], F32, name=f"result{m}_{c0}")
+                    single = keep.tile([P, width], F32, name=f"result{m}_{c0}", align_bytes=DMA_ALIGN)
                     result = single[:]
                 entries = offsets[:, c0 // GROUP : (c0 + width) // GROUP]
                 nc.vector.tensor_tensor(result, resid[m][:].indirect(entries), sums_at(c0, width), ADD)

@@ -36,7 +36,7 @@ SCALE_LOADS = [
 ]
 
 GROUP_WIDTHS = [[256, 256, 512], [512, 512], [512, 512], [512, 512]]
-ADD_WIDTHS = [[256, 256, 512], [1024], [1024], [512, 384, 128]]
+ADD_WIDTHS = [[256, 256, 512], [1024], [1024], [640, 384]]
 OPEN_BANKS = 4
 
 
@@ -102,7 +102,7 @@ def tile_list_tabres_none_kernel(
         for m in range(ROW_TILES):
             rows = slice(m * P, (m + 1) * P)
 
-            spans = [S] if ADD_WIDTHS[m] == [S] else GROUP_WIDTHS[m]
+            spans = GROUP_WIDTHS[m] if ADD_WIDTHS[m] == GROUP_WIDTHS[m] else [S]
             starts = [sum(spans[:i]) for i in range(len(spans))]
             sums = [keep.tile([P, span], F32, name=f"sums{m}_{i}") for i, span in enumerate(spans)]
 
@@ -146,7 +146,7 @@ def tile_list_tabres_none_kernel(
                 entries = offsets[:, c0 // GROUP : (c0 + width) // GROUP]
                 nc.vector.tensor_tensor(result, resid[m][:].indirect(entries), sums_at(c0, width), ADD)
                 if m >= JOINT_TILES:
-                    store_queue = nc.scalar if (m + piece) % 2 == 0 else nc.sync
+                    store_queue = nc.scalar if (m + piece) % 2 == 1 else nc.sync
                     store_queue.dma_start(out[rows, c0 : c0 + width], result)
                 c0 = c0 + width
             if m == JOINT_TILES - 1:

@@ -37,7 +37,7 @@ SCALE_LOADS = [
 
 GROUP_WIDTHS = [[256, 256, 512], [512, 512], [512, 512], [512, 512]]
 ADD_WIDTHS = [[256, 256, 512], [1024], [1024], [640, 384]]
-OPEN_BANKS = 4
+OPEN_BANKS = 6
 
 
 def tile_list_tabres_none_kernel(

@@ -36,7 +36,7 @@ SCALE_LOADS = [
 ]
 
 GROUP_WIDTHS = [[256, 256, 512], [512, 512], [512, 512], [512, 512]]
-ADD_WIDTHS = [[256, 256, 512], [1024], [1024], [640, 384]]
+ADD_WIDTHS = [[256, 256, 512], [1024], [1024], [512, 256, 256]]
 OPEN_BANKS = 6
 
 

@@ -36,7 +36,7 @@ SCALE_LOADS = [
 ]
 
 GROUP_WIDTHS = [[256, 256, 512], [512, 512], [512, 512], [512, 512]]
-ADD_WIDTHS = [[256, 256, 512], [1024], [1024], [512, 256, 256]]
+ADD_WIDTHS = [[256, 256, 512], [1024], [1024], [512, 320, 192]]
 OPEN_BANKS = 6
 
 
@@ -146,7 +146,7 @@ def tile_list_tabres_none_kernel(
                 entries = offsets[:, c0 // GROUP : (c0 + width) // GROUP]
                 nc.vector.tensor_tensor(result, resid[m][:].indirect(entries), sums_at(c0, width), ADD)
                 if m >= JOINT_TILES:
-                    store_queue = nc.scalar if (m + piece) % 2 == 1 else nc.sync
+                    store_queue = nc.scalar if (m + piece) % 2 == 0 else nc.sync
                     store_queue.dma_start(out[rows, c0 : c0 + width], result)
                 c0 = c0 + width
             if m == JOINT_TILES - 1:

from contextlib import ExitStack

import concourse.mybir as mybir

K, M, T, S = 1024, 512, 2048, 1024
FLOPS = 2 * K * M * S

F32 = mybir.dt.float32
BF16 = mybir.dt.bfloat16
I32 = mybir.dt.int32
U32 = mybir.dt.uint32
U16 = mybir.dt.uint16
U8 = mybir.dt.uint8
FP8X4 = mybir.dt.float8_e4m3fn_x4
FP4X4 = mybir.dt.float4_e2m1fn_x4
ADD = mybir.AluOpType.add

P = 128
QUADRANT = 32
PACK = 4
GROUP = 16
BANK = 512
DMA_ALIGN = 256
ROW_TILES = M // P
JOINT_TILES = 2

PLANE0 = 12

SCALE_LOADS = [
    ("sync", PLANE0, 0, 32),
    ("scalar", PLANE0 + QUADRANT, 4, 16),
    ("scalar", PLANE0 + QUADRANT + 16, 4 + 16, 8),
    ("sync", PLANE0 + 2 * QUADRANT - 8, 0, 32),
    ("sync", PLANE0 + 3 * QUADRANT, 12, PACK),
    ("sync", 0, 16, PACK),
]

GROUP_WIDTHS = [[256, 256, 512], [512, 512], [512, 512], [512, 512]]
ADD_WIDTHS = [[256, 256, 512], [1024], [1024], [512, 320, 192]]
OPEN_BANKS = 6


def tile_list_tabres_none_kernel(
    tc, tab_words, tab_scales, w8, w4_words, w4_scales, rT, offs, out
):
    nc = tc.nc
    queues = {"sync": nc.sync, "scalar": nc.scalar}
    with ExitStack() as ctx:
        keep = ctx.enter_context(tc.tile_pool(name="keep", bufs=1))
        psum = ctx.enter_context(tc.psum_pool(name="psum", bufs=OPEN_BANKS))

        offsets = keep.tile([P, S // GROUP], U16, name="offsets", align_bytes=DMA_ALIGN)
        scales = keep.tile([P, T // 4], I32, name="scales", align_bytes=DMA_ALIGN)
        w8_raw = keep.tile([P, PACK, M], F32, name="w8_raw", align_bytes=DMA_ALIGN)
        words = [keep.tile([P, T], I32, name=f"words{a}", align_bytes=DMA_ALIGN) for a in range(2)]
        w4_codes = keep.tile([P, 2 * M], U8, name="w4_codes", align_bytes=DMA_ALIGN)
        w4_plane = keep.tile([P, M // 4], I32, name="w4_plane", align_bytes=DMA_ALIGN)
        resid = [keep.tile([P, T], F32, name=f"resid{m}", align_bytes=DMA_ALIGN) for m in range(ROW_TILES)]

        nc.vector.memset(scales[3 * QUADRANT : P, :], 0)
        nc.vector.memset(scales[0:PLANE0, :], 0)

        table_words = [tab_words[a].rearrange("p t i -> p (t i)").bitcast(I32) for a in range(2)]
        scale_rows = tab_scales.rearrange("a q t -> (a q) t").bitcast(I32)
        w4_rows = w4_scales[0].bitcast(I32)
        w8_rows = w8.rearrange("(p j) n -> p j n", j=PACK)
        nc.sync.dma_start(offsets[:], offs)
        for queue, part, row, count in SCALE_LOADS:
            queues[queue].dma_start(scales[part : part + count, :], scale_rows[row : row + count, :])
        nc.sync.dma_start(words[1][:], table_words[1])
        nc.sync.dma_start(words[0][:], table_words[0])
        nc.sync.dma_start(w4_codes[:].bitcast(I32), w4_words[0].bitcast(I32))
        for r in range(PACK):
            nc.sync.dma_start(w4_plane[r:P:QUADRANT, :], w4_rows[r : PACK * PACK : PACK, :])
        nc.sync.dma_start(w8_raw[:], w8_rows)
        for m in range(ROW_TILES):
            nc.sync.dma_start(resid[m][:], rT[m * P : (m + 1) * P, :])

        picked_scales = keep.tile([P, S], U8, name="picked_scales", align_bytes=64)
        picked_words = [keep.tile([P, S], U32, name=f"picked_words{a}", align_bytes=64) for a in range(2)]
        nc.vector.tensor_copy(picked_scales[:], scales[:].bitcast(U8).indirect(offsets[:]))
        for a in (1, 0):
            nc.vector.tensor_copy(picked_words[a][:], words[a][:].bitcast(U32).indirect(offsets[:]))

        w8_codes = keep.tile([P, M], U32, name="w8_codes", align_bytes=64)
        w8_plane = keep.tile([P, M], U8, name="w8_plane", align_bytes=64)
        shares = [(0, P, nc.vector.tensor_copy), (P, P, nc.vector.tensor_copy), (2 * P, 2 * P, nc.scalar.copy)]
        for n0, count, interleave in shares:
            channels = slice(n0, n0 + count)
            grouped = keep.tile([P, count, PACK], BF16, name=f"grouped{n0}", align_bytes=64)
            interleave(
                grouped[:].rearrange("p (c i) t -> p c t i", i=4),
                w8_raw[:, :, channels].rearrange("p t (c i) -> p c t i", i=4),
            )
            nc.vector.quantize_mx(
                out=w8_codes[:, channels].bitcast(FP8X4),
                scales=w8_plane[:, channels],
                in_=grouped[:].rearrange("p c t -> p (c t)"),
            )

        joint = keep.tile([P, JOINT_TILES, S], F32, name="joint", align_bytes=DMA_ALIGN)
        for m in range(ROW_TILES):
            rows = slice(m * P, (m + 1) * P)

            spans = GROUP_WIDTHS[m] if ADD_WIDTHS[m] == GROUP_WIDTHS[m] else [S]
            starts = [sum(spans[:i]) for i in range(len(spans))]
            sums = [keep.tile([P, span], F32, name=f"sums{m}_{i}") for i, span in enumerate(spans)]

            def sums_at(first, width):
                i = max(i for i, start in enumerate(starts) if start <= first)
                return sums[i][:, first - starts[i] : first - starts[i] + width]

            g0 = 0
            for h, wide in enumerate(GROUP_WIDTHS[m]):
                bank = psum.tile([P, BANK], F32, name=f"acc{m}_{h}", tag="acc")
                step = BANK if wide == BANK else P
                for o in range(0, wide, step):
                    nc.tensor.matmul_mx(
                        out=bank[:, o : o + step],
                        lhsT=w4_codes[:, 2 * m * P : 2 * (m + 1) * P].bitcast(FP4X4),
                        lhsT_scale=w4_plane[:].bitcast(U8)[:, rows],
                        rhs=picked_words[1][:, g0 + o : g0 + o + step].bitcast(FP8X4),
                        rhs_scale=picked_scales[:, g0 + o : g0 + o + step],
                        start=o == 0,
                        stop=False,
                    )
                nc.tensor.matmul_mx(
                    out=bank[:, 0:wide],
                    lhsT=w8_codes[:, rows].bitcast(FP8X4),
                    lhsT_scale=w8_plane[:, rows],
                    rhs=picked_words[0][:, g0 : g0 + wide].bitcast(FP8X4),
                    rhs_scale=picked_scales[PLANE0:P, g0 : g0 + wide],
                    start=False,
                    stop=True,
                )
                nc.scalar.copy(sums_at(g0, wide), bank[:, 0:wide])
                g0 = g0 + wide

            c0 = 0
            for piece, width in enumerate(ADD_WIDTHS[m]):
                if m < JOINT_TILES:
                    result = joint[:, m, c0 : c0 + width]
                else:
                    single = keep.tile([P, width], F32, name=f"result{m}_{c0}", align_bytes=DMA_ALIGN)
                    result = single[:]
                entries = offsets[:, c0 // GROUP : (c0 + width) // GROUP]
                nc.vector.tensor_tensor(result, resid[m][:].indirect(entries), sums_at(c0, width), ADD)
                if m >= JOINT_TILES:
                    store_queue = nc.scalar if (m + piece) % 2 == 0 else nc.sync
                    store_queue.dma_start(out[rows, c0 : c0 + width], result)
                c0 = c0 + width
            if m == JOINT_TILES - 1:
                nc.sync.dma_start(out[0 : JOINT_TILES * P, :].rearrange("(m p) j -> p m j", p=P), joint[:])
